import numpy as np
import ml_dtypes


def mxq(x, axis, fmt="e4m3"):
    dtype, down = {"e4m3": (ml_dtypes.float8_e4m3fn, 7), "e5m2": (ml_dtypes.float8_e5m2, 14)}[fmt]
    v = np.moveaxis(np.asarray(x, np.float32).astype(ml_dtypes.bfloat16).astype(np.float64), axis, -1)
    blocks = v.reshape(v.shape[:-1] + (-1, 32))
    amax = np.abs(blocks).max(-1, keepdims=True)
    byte = np.maximum(np.where(amax > 0, np.frexp(amax)[1] - 1 + 127, 0) - down, 1)
    scale = np.exp2(byte - 127.0)
    codes = (blocks / scale).astype(np.float32).astype(dtype).astype(np.float64)
    return np.moveaxis((codes * scale).reshape(v.shape), -1, axis)


WIDE = False


def mx_kscale(k):
    if not WIDE:
        return np.ones(k)
    levels = np.array([10, -10, 5, -5, 0])
    if k % 512:
        return np.exp2(np.random.permutation(np.resize(levels, k // 32))).repeat(32)
    a = np.empty((k // 512, 16))
    for p in range(k // 512):
        a[p, :8] = np.random.permutation(np.resize(levels, 8))
        for g in range(8):
            far = levels[np.abs(levels - a[p, g]) >= 10]
            a[p, g + 8] = far[np.random.randint(len(far))]
    return np.exp2(a.ravel()).repeat(32)


BF16 = ml_dtypes.bfloat16


def bf(x):
    return np.asarray(x, np.float32).astype(BF16)


def f64(x):
    return np.asarray(x).astype(np.float64)


E2M1 = np.array([0.0, 0.5, 1.0, 1.5, 2.0, 3.0, 4.0, 6.0, -0.0, -0.5, -1.0, -1.5, -2.0, -3.0, -4.0, -6.0])


def pack_weight(w, fmt):
    k, n = w.shape
    w = f64(bf(w)).reshape(k // 32, 32, n)
    amax = np.abs(w).max(1)
    if fmt == "e4m3":
        byte = np.frexp(amax)[1] - 1 + 127 - 7
    else:
        mant, ex = np.frexp(amax / 6.0)
        byte = np.where(mant > 0.5, ex, ex - 1) + 127
    byte = np.clip(np.where(amax > 0, byte, 1), 1, 254)
    scaled = (w * np.exp2(127.0 - byte)[:, None, :]).reshape(k, n).astype(np.float32)
    by_word = np.ascontiguousarray(scaled.reshape(k // 512, 128, 4, n).transpose(0, 1, 3, 2))
    if fmt == "e4m3":
        words = by_word.astype(ml_dtypes.float8_e4m3fn).view(np.uint8)
    else:
        c = by_word.astype(ml_dtypes.float4_e2m1fn).view(np.uint8) & 0xF
        words = c[..., 0::2] | (c[..., 1::2] << 4)
    return np.ascontiguousarray(words), np.ascontiguousarray(byte.astype(np.uint8).reshape(k // 512, 16, n))


def unpack_weight(words, scales, fmt):
    g, p, n, _ = words.shape
    if fmt == "e4m3":
        vals = np.ascontiguousarray(words).view(ml_dtypes.float8_e4m3fn).astype(np.float64)
    else:
        nib = np.empty((g, p, n, 4), np.uint8)
        nib[..., 0::2] = words & 0xF
        nib[..., 1::2] = words >> 4
        vals = E2M1[nib]
    vals = vals * np.repeat(np.exp2(scales.astype(np.float64) - 127.0), 8, axis=1)[..., None]
    return vals.transpose(0, 1, 3, 2).reshape(g * 512, n)
def pack4(w):
    words, scales = pack_weight(w, "e2m1")
    return words.reshape(words.shape[0], 128, -1), scales


def unpack4(words, scales):
    return unpack_weight(words.reshape(words.shape[0], 128, -1, 2), scales, "e2m1")


M, N, K, C, F = 1024, 512, 1536, 2048, 1024


def draw0():
    s = mx_kscale(K)
    r = mx_kscale(C)
    u = mx_kscale(C)
    t = mx_kscale(F)
    v = np.random.standard_normal((C, F)) / np.sqrt(C) / r[:, None] * t
    v_words, v_scales = pack4(v)
    return {"act_train": bf(np.random.standard_normal((M, K)) * K ** -0.25 * s),
            "act_query": bf(np.random.standard_normal((N, K)) * K ** -0.25 / s),
            "err_train": bf(np.random.standard_normal((M, C)) * 2.0 * F ** -0.25 * r),
            "err_query": bf(np.random.standard_normal((N, C)) * 2.0 * F ** -0.25 * u),
            "slope_train": bf(1.0 / (1.0 + np.exp(-np.random.standard_normal((M, F))))),
            "slope_query": bf(1.0 / (1.0 + np.exp(-np.random.standard_normal((N, F))))),
            "v_words": v_words,
            "v_scales": v_scales,
            "w": bf(np.random.standard_normal((C, F)) / np.sqrt(C) / u[:, None] / t)}


def core(act_train, act_query, err_train, err_query, slope_train, slope_query, v_words, v_scales, w):
    back_train = mxq(f64(err_train), 1, "e4m3") @ unpack4(v_words, v_scales)
    back_query = mxq(f64(err_query), 1, "e4m3") @ mxq(f64(w), 0, "e4m3")
    d_train = back_train * f64(slope_train)
    d_query = back_query * f64(slope_query)
    gram_err = mxq(d_train, 1, "e4m3") @ mxq(d_query, 1, "e4m3").T
    gram_act = mxq(f64(act_train), 1, "e4m3") @ mxq(f64(act_query), 1, "e4m3").T
    return gram_act * gram_err


def e4m3fn_bytes(y):
    return np.clip(np.asarray(y, np.float64), -448.0, 448.0).astype(np.float32).astype(ml_dtypes.float8_e4m3fn).view(np.uint8)


def e4m3fn_values(b):
    return np.asarray(b, np.uint8).view(ml_dtypes.float8_e4m3fn).astype(np.float64)


def setup_inputs():
    d = draw0()
    x0 = np.asarray(d['err_train']).astype(np.float64)
    s = (np.max(np.abs(x0), axis=(0,), keepdims=True) / 448.0).astype(np.float32)
    out = {}
    for k, v in d.items():
        if k == 'err_train':
            out['err_train_bytes'] = e4m3fn_bytes(x0 / s.astype(np.float64))
            out['err_train_scale'] = s
        else:
            out[k] = v
    return out


def reference(act_train, act_query, err_train_bytes, err_train_scale, err_query, slope_train, slope_query, v_words, v_scales, w):
    return core(act_train, act_query, e4m3fn_values(err_train_bytes) * err_train_scale.astype(np.float64), err_query, slope_train, slope_query, v_words, v_scales, w)

@@ -1,0 +1,311 @@
+from contextlib import ExitStack
+
+import concourse.mybir as mybir
+from concourse.masks import make_identity
+
+M, N, K, C, F = 1024, 512, 1536, 2048, 1024
+P = 128
+FLOPS = 2 * (M * F * C + N * F * C + M * N * F + M * N * K)
+
+F32 = mybir.dt.float32
+BF16 = mybir.dt.bfloat16
+I32 = mybir.dt.int32
+U32 = mybir.dt.uint32
+U8 = mybir.dt.uint8
+FP8 = mybir.dt.float8_e4m3fn
+FP8X4 = mybir.dt.float8_e4m3fn_x4
+FP4X4 = mybir.dt.float4_e2m1fn_x4
+MULT = mybir.AluOpType.mult
+
+
+def tile_gradient_inner_products_s11_kernel(
+    tc, act_train, act_query, err_train_bytes, err_train_scale, err_query, slope_train, slope_query, v_words, v_scales, w, out
+):
+    nc = tc.nc
+    with ExitStack() as ctx:
+        keep = ctx.enter_context(tc.tile_pool(name="keep", bufs=1))
+        work = ctx.enter_context(tc.tile_pool(name="work", bufs=2))
+        psum = ctx.enter_context(tc.psum_pool(name="psum", bufs=4))
+        t = {}
+
+        def small(name, shape, dtype):
+            return keep.tile(shape, dtype, name=name, align_bytes=64)
+
+        ident = keep.tile([P, P], F32, name="ident", align_bytes=64)
+        make_identity(nc, ident[:])
+        v_planes = small("v_planes", [P, 4, F], U8)
+        nc.vector.memset(v_planes[:].rearrange("p g n -> p (g n)").bitcast(I32), 0)
+        v_codes = small("v_codes", [P, 4, 2 * F], U8)
+        scale = small("scale", [P, C], F32)
+        w_codes = small("w_codes", [P, 4, F], U32)
+        w_planes = small("w_planes", [P, 4, F], U8)
+        aq_codes = small("aq_codes", [P, 3, N], U32)
+        aq_planes = small("aq_planes", [P, 3, N], U8)
+        dq_codes = small("dq_codes", [P, 2, N], U32)
+        dq_planes = small("dq_planes", [P, 2, N], U8)
+        dt_codes = small("dt_codes", [P, 8, 2, P], U32)
+        dt_planes = small("dt_planes", [P, 8, 2, P], U8)
+        gram_act = small("gram_act", [P, 8, N], F32)
+
+        def load_act(src, name, i):
+            raw = work.tile([P, 2, K], BF16, tag="act_raw", name="act_raw", bufs=4, align_bytes=64)
+            view = src[256 * i : 256 * (i + 1), :].rearrange("(j p) k -> p j k", p=P)
+            if name == "aq":
+                for g in range(3):
+                    nc.sync.dma_start(out=raw[:, :, 512 * g : 512 * (g + 1)], in_=view[:, :, 512 * g : 512 * (g + 1)])
+            else:
+                nc.sync.dma_start(out=raw[:], in_=view)
+            t[name, i] = raw
+
+        def load_scale(h):
+            k = slice(1024 * h, 1024 * (h + 1))
+            nc.sync.dma_start(out=scale[:, k], in_=err_train_scale.rearrange("o k -> (o k)")[k].partition_broadcast(P))
+
+        def load_bytes(i):
+            b = small("bytes%d" % i, [P, 2, C], U8)
+            nc.sync.dma_start(out=b[:], in_=err_train_bytes[256 * i : 256 * (i + 1), :].rearrange("(j p) k -> p j k", p=P))
+            t["bytes", i] = b
+
+        def load_v():
+            for q in range(4):
+                nc.sync.dma_start(
+                    out=v_planes[32 * q : 32 * q + 4, :, :].bitcast(I32),
+                    in_=v_scales[:, 4 * q : 4 * q + 4, :].rearrange("g r n -> r g n").bitcast(I32),
+                )
+            nc.sync.dma_start(out=v_codes[:], in_=v_words.rearrange("g p b -> p g b"))
+
+        def load_w(g):
+            raw = work.tile([P, 4, F], BF16, tag="w_raw", name="w_raw", bufs=3, align_bytes=64)
+            nc.sync.dma_start(out=raw[:], in_=w[512 * g : 512 * (g + 1), :].rearrange("(p t) n -> p t n", t=4))
+            t["w", g] = raw
+
+        def load_err_query(i):
+            raw = small("errq%d" % i, [P, 2, C], BF16)
+            nc.sync.dma_start(out=raw[:], in_=err_query[256 * i : 256 * (i + 1), :].rearrange("(j p) k -> p j k", p=P))
+            t["errq", i] = raw
+
+        def load_slope(name, i):
+            src = slope_train if name == "e" else slope_query
+            s = work.tile([P, 2, F], BF16, tag="slope", name="slope", bufs=4, align_bytes=64)
+            nc.sync.dma_start(out=s[:], in_=src[256 * i : 256 * (i + 1), :].rearrange("(j p) k -> p j k", p=P))
+            t["slope", name, 2 * i] = s[:, 0, :]
+            t["slope", name, 2 * i + 1] = s[:, 1, :]
+
+        def turn(key, parts):
+            bank = psum.tile([P, 4, P], F32, tag="turn", name="turn", bufs=4)
+            for j, words in enumerate(parts):
+                nc.tensor.transpose(bank[:, j, :], words, ident[:])
+            t["bank", key] = bank
+
+        def evac(key):
+            x = work.tile([P, 2, P, 4], BF16, tag="kx", name="kx", bufs=5, align_bytes=64)
+            nc.scalar.copy(out=x[:].bitcast(F32), in_=t["bank", key][:].rearrange("p (g u) r -> p g r u", g=2))
+            t["kx", key] = x
+
+        def quant(key, codes, planes):
+            nc.vector.quantize_mx(out=codes.bitcast(FP8X4), scales=planes, in_=t["kx", key][:].rearrange("p g r t -> p (g r t)"))
+
+        def second(words, g):
+            return [words[:, 256 * g + u : 256 * (g + 1) : 2] for u in range(2)]
+
+        def turn_act(name, i, g):
+            raw = t[name, i]
+            turn((name, i, g), second(raw[:, 0, :].bitcast(F32), g) + second(raw[:, 1, :].bitcast(F32), g))
+
+        def evac_act(name, i, g):
+            evac((name, i, g))
+
+        def quant_act(name, i, g):
+            if name == "aq":
+                quant((name, i, g), aq_codes[:, g, 256 * i : 256 * (i + 1)], aq_planes[:, g, 256 * i : 256 * (i + 1)])
+            else:
+                if g == 0:
+                    t["at_codes", i] = work.tile([P, 3, 2 * P], U32, tag="at_codes", name="at_codes", align_bytes=64)
+                    t["at_planes", i] = work.tile([P, 3, 2 * P], U8, tag="at_planes", name="at_planes", align_bytes=64)
+                quant((name, i, g), t["at_codes", i][:, g, :], t["at_planes", i][:, g, :])
+
+        def mm_act(i):
+            acc = psum.tile([P, N], F32, tag="acc", name="acc", bufs=4)
+            half = slice(P * (i % 2), P * (i % 2) + P)
+            for g in range(3):
+                nc.tensor.matmul_mx(
+                    out=acc[:], lhsT=t["at_codes", i // 2][:, g, half].bitcast(FP8X4), lhsT_scale=t["at_planes", i // 2][:, g, half],
+                    rhs=aq_codes[:, g, :].bitcast(FP8X4), rhs_scale=aq_planes[:, g, :], start=g == 0, stop=g == 2,
+                )
+            t["gram", i] = acc
+
+        def keep_gram(i):
+            nc.scalar.copy(out=gram_act[:, i, :], in_=t["gram", i][:])
+
+        def scale_err(i, h):
+            if h == 0:
+                t["err", "e", i] = work.tile([P, C], BF16, tag="err", name="err", bufs=3, align_bytes=64)
+            k = slice(1024 * h, 1024 * (h + 1))
+            nc.vector.tensor_tensor(out=t["err", "e", i][:, k], in0=t["bytes", i // 2][:, i % 2, k].bitcast(FP8), in1=scale[:, k], op=MULT)
+
+        def turn_err(name, i, b):
+            words = t["err", "e", i][:].bitcast(F32) if name == "e" else t["errq", i // 2][:, i % 2, :].bitcast(F32)
+            turn((name, i, b), second(words, 2 * b) + second(words, 2 * b + 1))
+
+        def evac_err(name, i, b):
+            evac((name, i, b))
+
+        def quant_err(name, i, b):
+            if b == 0:
+                t["codes", name, i] = work.tile([P, 4, P], U32, tag="e_codes", name="e_codes", bufs=3, align_bytes=64)
+                t["planes", name, i] = work.tile([P, 4, P], U8, tag="e_planes", name="e_planes", bufs=3, align_bytes=64)
+            quant((name, i, b), t["codes", name, i][:, 2 * b : 2 * b + 2, :].rearrange("p g r -> p (g r)"), t["planes", name, i][:, 2 * b : 2 * b + 2, :].rearrange("p g r -> p (g r)"))
+
+        def mm_err(name, i, h):
+            acc = psum.tile([P, N], F32, tag="acc", name="acc", bufs=4)
+            for g in range(4):
+                if name == "e":
+                    rhs, rhs_scale = v_codes[:, g, 1024 * h : 1024 * (h + 1)].bitcast(FP4X4), v_planes[:, g, 512 * h : 512 * (h + 1)]
+                else:
+                    rhs, rhs_scale = w_codes[:, g, 512 * h : 512 * (h + 1)].bitcast(FP8X4), w_planes[:, g, 512 * h : 512 * (h + 1)]
+                nc.tensor.matmul_mx(
+                    out=acc[:], lhsT=t["codes", name, i][:, g, :].bitcast(FP8X4), lhsT_scale=t["planes", name, i][:, g, :],
+                    rhs=rhs, rhs_scale=rhs_scale, start=g == 0, stop=g == 3,
+                )
+            t["back", name, i, h] = acc
+
+        def slope_mul(name, i, h):
+            if h == 0:
+                t["d", name, i] = work.tile([P, 2, 2, P, 2], BF16, tag="d", name="d", bufs=3, align_bytes=64)
+            nc.vector.tensor_tensor(
+                out=t["d", name, i][:, h],
+                in0=t["back", name, i, h][:].rearrange("p (m u e) -> p u m e", u=2, e=2),
+                in1=t["slope", name, i][:, 512 * h : 512 * (h + 1)].rearrange("p (m u e) -> p u m e", u=2, e=2),
+                op=MULT,
+            )
+
+        def turn_d(name, i):
+            words = t["d", name, i][:].rearrange("p h u m e -> p (h u m e)").bitcast(F32)
+            turn(("d", name, i), [words[:, P * j : P * (j + 1)] for j in range(4)])
+
+        def evac_d(name, i):
+            evac(("d", name, i))
+
+        def quant_d(name, i):
+            if name == "e":
+                quant(("d", name, i), dt_codes[:, i].rearrange("p g r -> p (g r)"), dt_planes[:, i].rearrange("p g r -> p (g r)"))
+            else:
+                x = t["kx", ("d", name, i)]
+                for g in range(2):
+                    nc.vector.quantize_mx(
+                        out=dq_codes[:, g, P * i : P * (i + 1)].bitcast(FP8X4), scales=dq_planes[:, g, P * i : P * (i + 1)],
+                        in_=x[:, g].rearrange("p r t -> p (r t)"),
+                    )
+
+        def w_lay(c, engine):
+            g, n0 = c // 4, 256 * (c % 4)
+            x = work.tile([P, 256, 4], BF16, tag="wx", name="wx", bufs=4, align_bytes=64)
+            dst = x[:].rearrange("p (c i) t -> p c t i", i=4)
+            src = t["w", g][:, :, n0 : n0 + 256].rearrange("p t (c i) -> p c t i", i=4)
+            if engine == "act":
+                nc.scalar.copy(out=dst, in_=src)
+            else:
+                nc.vector.tensor_copy(out=dst, in_=src)
+            t["wx", c] = x
+
+        def w_quant(c):
+            g, n0 = c // 4, 256 * (c % 4)
+            nc.vector.quantize_mx(
+                out=w_codes[:, g, n0 : n0 + 256].bitcast(FP8X4), scales=w_planes[:, g, n0 : n0 + 256],
+                in_=t["wx", c][:].rearrange("p n t -> p (n t)"),
+            )
+
+        def mm_gram(i):
+            acc = psum.tile([P, N], F32, tag="acc", name="acc", bufs=4)
+            for g in range(2):
+                nc.tensor.matmul_mx(
+                    out=acc[:], lhsT=dt_codes[:, i, g, :].bitcast(FP8X4), lhsT_scale=dt_planes[:, i, g, :],
+                    rhs=dq_codes[:, g, :].bitcast(FP8X4), rhs_scale=dq_planes[:, g, :], start=g == 0, stop=g == 1,
+                )
+            t["ge", i] = acc
+
+        def finish(i):
+            res = work.tile([P, N], F32, tag="res", name="res", bufs=2, align_bytes=64)
+            nc.vector.tensor_tensor(out=res[:], in0=t["ge", i][:], in1=gram_act[:, i, :], op=MULT)
+            nc.sync.dma_start(out=out[P * i : P * (i + 1), :], in_=res[:])
+
+        for fn, a in [
+            (load_scale, (0,)),
+            (load_bytes, (0,)),
+            (load_scale, (1,)),
+            (load_act, (act_query, "aq", 0)),
+            (load_bytes, (1,)),
+            (load_act, (act_train, "at", 0)),
+            (load_v, ()),
+            (load_w, (0,)),
+            (load_slope, ("e", 0)),
+            (load_bytes, (2,)),
+            (load_act, (act_query, "aq", 1)),
+            (load_act, (act_train, "at", 1)),
+            (load_slope, ("e", 1)),
+            (load_slope, ("e", 2)),
+            (load_w, (1,)),
+            (load_w, (2,)),
+            (load_act, (act_train, "at", 2)),
+            (load_slope, ("r", 0)),
+            (load_err_query, (0,)),
+            (load_slope, ("r", 1)),
+            (load_bytes, (3,)),
+            (load_w, (3,)),
+            (load_slope, ("e", 3)),
+            (load_err_query, (1,)),
+            (load_act, (act_train, "at", 3)),
+        ]:
+            fn(*a)
+
+        waiting = []
+        count = {"lay": 0, "quant": 0}
+
+        def settle(q, n):
+            while len(q) > n:
+                fn, a = q[0]
+                q.remove(q[0])
+                fn(*a)
+
+        ORDER = """
+            q00 s0a s0b s1a s1b q01 e00 e01 s2a s2b q02 e10 e11 a00 a01 a02 e20 s3a e21 B00 B01 s3b wl s4a
+            B10 s4b wl B11 wl wq B20 e30 q10 q11 wq e31 a10 e40 s5a q12 d0 e41 wq wl B21 B30 a11 A0
+            wl A1 wq s5b wq B31 wv wl wl wq B40 wv B41 wq d1 a12 e50 a20 e51 wq r00 wl wv wq
+            d2 wv wq r01 wv r10 a21 A2 B50 wq wq wl wv A3 wv wq wq B51 wq r11 wq a22 r20 a30
+            r21 d3 d4 s6a R00 A4 R01 s6b R10 R11 r30 x0 r31 d5 s7a x1 R20 R21 R30 s7b R31 e60 x2 e61
+            a31 x3 e70 a32 e71 B60 G0 A5 B61 G1 G2 B70 B71 G3 A6 d6 d7 A7 G4 G5 G6 G7
+        """
+        using = []
+        TURNS = {
+            "q": (turn_act, evac_act, quant_act, ("aq",)), "a": (turn_act, evac_act, quant_act, ("at",)),
+            "e": (turn_err, evac_err, quant_err, ("e",)), "r": (turn_err, evac_err, quant_err, ("r",)),
+            "d": (turn_d, evac_d, quant_d, ("e",)), "x": (turn_d, evac_d, quant_d, ("r",)),
+        }
+        PRODUCTS = {"A": (mm_act, keep_gram, ()), "B": (mm_err, slope_mul, ("e",)), "R": (mm_err, slope_mul, ("r",)), "G": (mm_gram, finish, ())}
+        with tc.manual_schedule():
+            for item in ORDER.split():
+                kind = item[0]
+                if item in ("wl", "wv"):
+                    w_lay(count["lay"], "act" if item == "wl" else "dve")
+                    count["lay"] += 1
+                elif item == "wq":
+                    w_quant(count["quant"])
+                    count["quant"] += 1
+                elif kind == "s":
+                    scale_err(int(item[1]), "ab".index(item[2]))
+                elif kind in TURNS:
+                    settle(using, 0)
+                    turn_fn, evac_fn, quant_fn, first = TURNS[kind]
+                    a = first + tuple([int(z) for z in item[1:]])
+                    turn_fn(*a)
+                    evac_fn(*a)
+                    waiting.append((quant_fn, a))
+                    settle(waiting, 1)
+                else:
+                    settle(using, 0)
+                    settle(waiting, 0)
+                    mm, use, first = PRODUCTS[kind]
+                    a = first + tuple([int(z) for z in item[1:]])
+                    mm(*a)
+                    using.append((use, a))
+            settle(using, 0)

@@ -108,9 +108,27 @@ def tile_gradient_inner_products_s11_kernel(
         def second(words, g):
             return [words[:, 256 * g + u : 256 * (g + 1) : 2] for u in range(2)]
 
+        def sorted_words(key):
+            x = t["sorted", key]
+            return [x[:, j, u, :] for j in range(2) for u in range(2)]
+
+        def sort_words(key, src):
+            x = work.tile([P, 2, 2, P], F32, tag="sorted", name="sorted", bufs=3, align_bytes=64)
+            nc.scalar.copy(out=x[:], in_=src)
+            t["sorted", key] = x
+
+        def sort_act(name, i, g):
+            sort_words((name, i, g), t[name, i][:, :, 512 * g : 512 * (g + 1)].bitcast(F32).rearrange("p j (m u) -> p j u m", u=2))
+
+        def sort_err(i, b):
+            sort_words(("r", i, b), t["errq", i // 2][:, i % 2, 1024 * b : 1024 * (b + 1)].bitcast(F32).rearrange("p (g m u) -> p g u m", g=2, u=2))
+
         def turn_act(name, i, g):
             raw = t[name, i]
-            turn((name, i, g), second(raw[:, 0, :].bitcast(F32), g) + second(raw[:, 1, :].bitcast(F32), g))
+            if ("sorted", (name, i, g)) in t:
+                turn((name, i, g), sorted_words((name, i, g)))
+            else:
+                turn((name, i, g), second(raw[:, 0, :].bitcast(F32), g) + second(raw[:, 1, :].bitcast(F32), g))
 
         def evac_act(name, i, g):
             evac((name, i, g))
@@ -145,7 +163,10 @@ def tile_gradient_inner_products_s11_kernel(
 
         def turn_err(name, i, b):
             words = t["err", "e", i][:].bitcast(F32) if name == "e" else t["errq", i // 2][:, i % 2, :].bitcast(F32)
-            turn((name, i, b), second(words, 2 * b) + second(words, 2 * b + 1))
+            if ("sorted", (name, i, b)) in t:
+                turn((name, i, b), sorted_words((name, i, b)))
+            else:
+                turn((name, i, b), second(words, 2 * b) + second(words, 2 * b + 1))
 
         def evac_err(name, i, b):
             evac((name, i, b))
@@ -230,31 +251,31 @@ def tile_gradient_inner_products_s11_kernel(
             nc.sync.dma_start(out=out[P * i : P * (i + 1), :], in_=res[:])
 
         for fn, a in [
-            (load_scale, (0,)),
             (load_bytes, (0,)),
+            (load_scale, (0,)),
             (load_scale, (1,)),
             (load_act, (act_query, "aq", 0)),
             (load_bytes, (1,)),
             (load_act, (act_train, "at", 0)),
             (load_v, ()),
+            (load_act, (act_query, "aq", 1)),
+            (load_bytes, (2,)),
             (load_w, (0,)),
             (load_slope, ("e", 0)),
-            (load_bytes, (2,)),
-            (load_act, (act_query, "aq", 1)),
-            (load_act, (act_train, "at", 1)),
             (load_slope, ("e", 1)),
-            (load_slope, ("e", 2)),
+            (load_act, (act_train, "at", 1)),
             (load_w, (1,)),
+            (load_slope, ("e", 2)),
+            (load_bytes, (3,)),
+            (load_err_query, (0,)),
             (load_w, (2,)),
             (load_act, (act_train, "at", 2)),
-            (load_slope, ("r", 0)),
-            (load_err_query, (0,)),
-            (load_slope, ("r", 1)),
-            (load_bytes, (3,)),
-            (load_w, (3,)),
-            (load_slope, ("e", 3)),
             (load_err_query, (1,)),
+            (load_w, (3,)),
             (load_act, (act_train, "at", 3)),
+            (load_slope, ("r", 0)),
+            (load_slope, ("r", 1)),
+            (load_slope, ("e", 3)),
         ]:
             fn(*a)
 
@@ -268,12 +289,13 @@ def tile_gradient_inner_products_s11_kernel(
                 fn(*a)
 
         ORDER = """
-            q00 s0a s0b s1a s1b q01 e00 e01 s2a s2b q02 e10 e11 a00 a01 a02 e20 s3a e21 B00 B01 s3b wl s4a
-            B10 s4b wl B11 wl wq B20 e30 q10 q11 wq e31 a10 e40 s5a q12 d0 e41 wq wl B21 B30 a11 A0
-            wl A1 wq s5b wq B31 wv wl wl wq B40 wv B41 wq d1 a12 e50 a20 e51 wq r00 wl wv wq
-            d2 wv wq r01 wv r10 a21 A2 B50 wq wq wl wv A3 wv wq wq B51 wq r11 wq a22 r20 a30
-            r21 d3 d4 s6a R00 A4 R01 s6b R10 R11 r30 x0 r31 d5 s7a x1 R20 R21 R30 s7b R31 e60 x2 e61
-            a31 x3 e70 a32 e71 B60 G0 A5 B61 G1 G2 B70 B71 G3 A6 d6 d7 A7 G4 G5 G6 G7
+            s0a s0b s1a s1b q00 q01 e00 e01 s2a e10 s2b s3a q02 e11 a00 e20 s3b a01 pq a02 s4a e21 e30 pq
+            B00 s4b B01 pq B10 B11 wl wl q10 s5a wq e31 wl e40 wl B20 B21 a10 s5b pa d0 wq e41 B30
+            q11 wq wv pa e50 wq wl B31 wv q12 d1 wq d2 wv wq e51 wl B40 B41 a11 pa r00 wq d3
+            pa wq wq wv r01 a12 B50 wq B51 wv wv wl A0 wv A1 wq d4 wq a20 wv wq wq wv wq
+            pa pr wq r10 r11 a21 pr A2 pr s6a A3 r20 r21 a22 R00 pa R01 s6b s7a pa R10 e60 r30 r31
+            R11 R20 e61 d5 a30 pa x0 R21 R30 R31 s7b B60 B61 x1 e70 e71 x2 x3 A4 a31 a32 d6 A5 B70
+            G0 G1 B71 G2 A6 G3 d7 G4 G5 A7 G6 G7
         """
         using = []
         TURNS = {
@@ -282,10 +304,18 @@ def tile_gradient_inner_products_s11_kernel(
             "d": (turn_d, evac_d, quant_d, ("e",)), "x": (turn_d, evac_d, quant_d, ("r",)),
         }
         PRODUCTS = {"A": (mm_act, keep_gram, ()), "B": (mm_err, slope_mul, ("e",)), "R": (mm_err, slope_mul, ("r",)), "G": (mm_gram, finish, ())}
+        PREPS = {"q": list(range(3, 6)), "a": list(range(4, 12)), "r": list(range(5, 8))}
         with tc.manual_schedule():
             for item in ORDER.split():
                 kind = item[0]
-                if item in ("wl", "wv"):
+                if kind == "p":
+                    i = PREPS[item[1]][0]
+                    PREPS[item[1]].remove(i)
+                    if item[1] == "r":
+                        sort_err(i // 2, i % 2)
+                    else:
+                        sort_act("aq" if item[1] == "q" else "at", i // 3, i % 3)
+                elif item in ("wl", "wv"):
                     w_lay(count["lay"], "act" if item == "wl" else "dve")
                     count["lay"] += 1
                 elif item == "wq":

@@ -50,16 +50,25 @@ def tile_gradient_inner_products_s11_kernel(
         def load_act(src, name, i):
             raw = work.tile([P, 2, K], BF16, tag="act_raw", name="act_raw", bufs=4, align_bytes=64)
             view = src[256 * i : 256 * (i + 1), :].rearrange("(j p) k -> p j k", p=P)
-            if name == "aq":
+            if name == "aq" or i == 0:
                 for g in range(3):
                     nc.sync.dma_start(out=raw[:, :, 512 * g : 512 * (g + 1)], in_=view[:, :, 512 * g : 512 * (g + 1)])
             else:
                 nc.sync.dma_start(out=raw[:], in_=view)
             t[name, i] = raw
 
-        def load_scale(h):
-            k = slice(1024 * h, 1024 * (h + 1))
-            nc.sync.dma_start(out=scale[:, k], in_=err_train_scale.rearrange("o k -> (o k)")[k].partition_broadcast(P))
+        def spread_scale():
+            rows = small("scale_rows", [P, 2, 32], F32)
+            cols = small("scale_cols", [P, 2, 32], F32)
+            for q in range(4):
+                nc.scalar.dma_start(out=rows[32 * q : 32 * q + 32], in_=err_train_scale.rearrange("o (h b j) -> (o b) h j", h=2, b=32))
+            for h in range(2):
+                nc.vector.transpose(out=cols[:, h, :], in_=rows[:, h, :])
+            flat = cols[:].rearrange("p h b -> p (h b)")
+            for c in range(4):
+                x = work.tile([P, 16, 32], F32, tag="wx", name="spread", bufs=4, align_bytes=64)
+                nc.scalar.copy(out=x[:], in_=flat[:, 16 * c : 16 * c + 16].unsqueeze(2).to_broadcast([P, 16, 32]))
+                nc.vector.transpose(out=scale[:, 512 * c : 512 * (c + 1)], in_=x[:].rearrange("p b i -> p (b i)"))
 
         def load_bytes(i):
             b = small("bytes%d" % i, [P, 2, C], U8)
@@ -246,35 +255,33 @@ def tile_gradient_inner_products_s11_kernel(
             t["ge", i] = acc
 
         def finish(i):
-            res = work.tile([P, N], F32, tag="res", name="res", bufs=2, align_bytes=64)
+            res = work.tile([P, N], F32, tag="wx", name="res", bufs=4, align_bytes=64)
             nc.vector.tensor_tensor(out=res[:], in0=t["ge", i][:], in1=gram_act[:, i, :], op=MULT)
             nc.sync.dma_start(out=out[P * i : P * (i + 1), :], in_=res[:])
 
         for fn, a in [
-            (load_bytes, (0,)),
-            (load_scale, (0,)),
-            (load_scale, (1,)),
             (load_act, (act_query, "aq", 0)),
-            (load_bytes, (1,)),
-            (load_act, (act_train, "at", 0)),
-            (load_v, ()),
+            (load_bytes, (0,)),
             (load_act, (act_query, "aq", 1)),
-            (load_bytes, (2,)),
-            (load_w, (0,)),
-            (load_slope, ("e", 0)),
-            (load_slope, ("e", 1)),
+            (load_act, (act_train, "at", 0)),
             (load_act, (act_train, "at", 1)),
+            (load_act, (act_train, "at", 2)),
+            (load_w, (0,)),
+            (load_bytes, (1,)),
+            (load_bytes, (2,)),
+            (load_v, ()),
             (load_w, (1,)),
+            (load_slope, ("e", 0)),
+            (load_err_query, (0,)),
+            (load_slope, ("r", 0)),
+            (load_act, (act_train, "at", 3)),
+            (load_w, (2,)),
+            (load_slope, ("e", 1)),
+            (load_slope, ("r", 1)),
+            (load_err_query, (1,)),
             (load_slope, ("e", 2)),
             (load_bytes, (3,)),
-            (load_err_query, (0,)),
-            (load_w, (2,)),
-            (load_act, (act_train, "at", 2)),
-            (load_err_query, (1,)),
             (load_w, (3,)),
-            (load_act, (act_train, "at", 3)),
-            (load_slope, ("r", 0)),
-            (load_slope, ("r", 1)),
             (load_slope, ("e", 3)),
         ]:
             fn(*a)
@@ -289,13 +296,13 @@ def tile_gradient_inner_products_s11_kernel(
                 fn(*a)
 
         ORDER = """
-            s0a s0b s1a s1b q00 q01 e00 e01 s2a e10 s2b s3a q02 e11 a00 e20 s3b a01 pq a02 s4a e21 e30 pq
-            B00 s4b B01 pq B10 B11 wl wl q10 s5a wq e31 wl e40 wl B20 B21 a10 s5b pa d0 wq e41 B30
-            q11 wq wv pa e50 wq wl B31 wv q12 d1 wq d2 wv wq e51 wl B40 B41 a11 pa r00 wq d3
-            pa wq wq wv r01 a12 B50 wq B51 wv wv wl A0 wv A1 wq d4 wq a20 wv wq wq wv wq
-            pa pr wq r10 r11 a21 pr A2 pr s6a A3 r20 r21 a22 R00 pa R01 s6b s7a pa R10 e60 r30 r31
-            R11 R20 e61 d5 a30 pa x0 R21 R30 R31 s7b B60 B61 x1 e70 e71 x2 x3 A4 a31 a32 d6 A5 B70
-            G0 G1 B71 G2 A6 G3 d7 G4 G5 A7 G6 G7
+            q00 q01 q02 s0a q10 q11 q12 a00 a01 s0b a02 s1a e00 a10 a11 a12 pa s1b s2a a20 e01 wl a21 e10
+            s2b A0 A1 a22 wv wq s3a s3b wl e11 e20 A2 wl A3 B00 wq B01 e21 wl s4a e30 e31 wq wq
+            s4b wl A4 B10 B11 B20 wq wl pr s5a d0 wq s5b e40 e41 B21 wq wv wl wl pr B30 wq B31
+            wq wv wq e50 r00 e51 d1 wq B40 wl wq pr B41 wv r01 wq r10 wl wq wv r11 pr wq d2
+            wl wq A5 B50 B51 r20 r21 d3 pa s6a s6b d4 R00 R01 R10 pr pr R11 r30 r31 e60 pa s7a e61
+            a30 pa R20 R21 a31 d5 s7b a32 x0 R30 R31 B60 x1 e70 x2 e71 x3 A6 B61 B70 G0 B71 G1 G2
+            G3 d6 d7 G4 G5 A7 G6 G7
         """
         using = []
         TURNS = {
@@ -304,8 +311,9 @@ def tile_gradient_inner_products_s11_kernel(
             "d": (turn_d, evac_d, quant_d, ("e",)), "x": (turn_d, evac_d, quant_d, ("r",)),
         }
         PRODUCTS = {"A": (mm_act, keep_gram, ()), "B": (mm_err, slope_mul, ("e",)), "R": (mm_err, slope_mul, ("r",)), "G": (mm_gram, finish, ())}
-        PREPS = {"q": list(range(3, 6)), "a": list(range(4, 12)), "r": list(range(5, 8))}
+        PREPS = {"q": list(range(6, 6)), "a": list(range(8, 12)), "r": list(range(2, 8))}
         with tc.manual_schedule():
+            spread_scale()
             for item in ORDER.split():
                 kind = item[0]
                 if kind == "p":

from contextlib import ExitStack

import concourse.mybir as mybir
from concourse.masks import make_identity

M, N, K, C, F = 1024, 512, 1536, 2048, 1024
P = 128
FLOPS = 2 * (M * F * C + N * F * C + M * N * F + M * N * K)

F32 = mybir.dt.float32
BF16 = mybir.dt.bfloat16
I32 = mybir.dt.int32
U32 = mybir.dt.uint32
U8 = mybir.dt.uint8
FP8 = mybir.dt.float8_e4m3fn
FP8X4 = mybir.dt.float8_e4m3fn_x4
FP4X4 = mybir.dt.float4_e2m1fn_x4
MULT = mybir.AluOpType.mult


def tile_gradient_inner_products_s11_kernel(
    tc, act_train, act_query, err_train_bytes, err_train_scale, err_query, slope_train, slope_query, v_words, v_scales, w, out
):
    nc = tc.nc
    with ExitStack() as ctx:
        keep = ctx.enter_context(tc.tile_pool(name="keep", bufs=1))
        work = ctx.enter_context(tc.tile_pool(name="work", bufs=2))
        psum = ctx.enter_context(tc.psum_pool(name="psum", bufs=4))
        t = {}

        def small(name, shape, dtype):
            return keep.tile(shape, dtype, name=name, align_bytes=64)

        ident = keep.tile([P, P], F32, name="ident", align_bytes=64)
        make_identity(nc, ident[:])
        v_planes = small("v_planes", [P, 4, F], U8)
        nc.vector.memset(v_planes[:].rearrange("p g n -> p (g n)").bitcast(I32), 0)
        v_codes = small("v_codes", [P, 4, 2 * F], U8)
        scale = small("scale", [P, C], F32)
        w_codes = small("w_codes", [P, 4, F], U32)
        w_planes = small("w_planes", [P, 4, F], U8)
        aq_codes = small("aq_codes", [P, 3, N], U32)
        aq_planes = small("aq_planes", [P, 3, N], U8)
        dq_codes = small("dq_codes", [P, 2, N], U32)
        dq_planes = small("dq_planes", [P, 2, N], U8)
        dt_codes = small("dt_codes", [P, 8, 2, P], U32)
        dt_planes = small("dt_planes", [P, 8, 2, P], U8)
        gram_act = small("gram_act", [P, 8, N], F32)

        def load_act(src, name, i):
            raw = work.tile([P, 2, K], BF16, tag="act_raw", name="act_raw", bufs=4, align_bytes=64)
            view = src[256 * i : 256 * (i + 1), :].rearrange("(j p) k -> p j k", p=P)
            if name == "aq" or i == 0:
                for g in range(3):
                    nc.sync.dma_start(out=raw[:, :, 512 * g : 512 * (g + 1)], in_=view[:, :, 512 * g : 512 * (g + 1)])
            else:
                nc.sync.dma_start(out=raw[:], in_=view)
            t[name, i] = raw

        def spread_scale():
            rows = small("scale_rows", [P, 2, 32], F32)
            cols = small("scale_cols", [P, 2, 32], F32)
            for q in range(4):
                nc.scalar.dma_start(out=rows[32 * q : 32 * q + 32], in_=err_train_scale.rearrange("o (h b j) -> (o b) h j", h=2, b=32))
            for h in range(2):
                nc.vector.transpose(out=cols[:, h, :], in_=rows[:, h, :])
            flat = cols[:].rearrange("p h b -> p (h b)")
            for c in range(4):
                x = work.tile([P, 16, 32], F32, tag="wx", name="spread", bufs=4, align_bytes=64)
                nc.scalar.copy(out=x[:], in_=flat[:, 16 * c : 16 * c + 16].unsqueeze(2).to_broadcast([P, 16, 32]))
                nc.vector.transpose(out=scale[:, 512 * c : 512 * (c + 1)], in_=x[:].rearrange("p b i -> p (b i)"))

        def load_bytes(i):
            b = small("bytes%d" % i, [P, 2, C], U8)
            nc.sync.dma_start(out=b[:], in_=err_train_bytes[256 * i : 256 * (i + 1), :].rearrange("(j p) k -> p j k", p=P))
            t["bytes", i] = b

        def load_v():
            for q in range(4):
                nc.sync.dma_start(
                    out=v_planes[32 * q : 32 * q + 4, :, :].bitcast(I32),
                    in_=v_scales[:, 4 * q : 4 * q + 4, :].rearrange("g r n -> r g n").bitcast(I32),
                )
            nc.sync.dma_start(out=v_codes[:], in_=v_words.rearrange("g p b -> p g b"))

        def load_w(g):
            raw = work.tile([P, 4, F], BF16, tag="w_raw", name="w_raw", bufs=3, align_bytes=64)
            nc.sync.dma_start(out=raw[:], in_=w[512 * g : 512 * (g + 1), :].rearrange("(p t) n -> p t n", t=4))
            t["w", g] = raw

        def load_err_query(i):
            raw = small("errq%d" % i, [P, 2, C], BF16)
            nc.sync.dma_start(out=raw[:], in_=err_query[256 * i : 256 * (i + 1), :].rearrange("(j p) k -> p j k", p=P))
            t["errq", i] = raw

        def load_slope(name, i):
            src = slope_train if name == "e" else slope_query
            s = work.tile([P, 2, F], BF16, tag="slope", name="slope", bufs=4, align_bytes=64)
            nc.sync.dma_start(out=s[:], in_=src[256 * i : 256 * (i + 1), :].rearrange("(j p) k -> p j k", p=P))
            t["slope", name, 2 * i] = s[:, 0, :]
            t["slope", name, 2 * i + 1] = s[:, 1, :]

        def turn(key, parts):
            bank = psum.tile([P, 4, P], F32, tag="turn", name="turn", bufs=4)
            for j, words in enumerate(parts):
                nc.tensor.transpose(bank[:, j, :], words, ident[:])
            t["bank", key] = bank

        def evac(key):
            x = work.tile([P, 2, P, 4], BF16, tag="kx", name="kx", bufs=5, align_bytes=64)
            nc.scalar.copy(out=x[:].bitcast(F32), in_=t["bank", key][:].rearrange("p (g u) r -> p g r u", g=2))
            t["kx", key] = x

        def quant(key, codes, planes):
            nc.vector.quantize_mx(out=codes.bitcast(FP8X4), scales=planes, in_=t["kx", key][:].rearrange("p g r t -> p (g r t)"))

        def second(words, g):
            return [words[:, 256 * g + u : 256 * (g + 1) : 2] for u in range(2)]

        def sorted_words(key):
            x = t["sorted", key]
            return [x[:, j, u, :] for j in range(2) for u in range(2)]

        def sort_words(key, src):
            x = work.tile([P, 2, 2, P], F32, tag="sorted", name="sorted", bufs=3, align_bytes=64)
            nc.scalar.copy(out=x[:], in_=src)
            t["sorted", key] = x

        def sort_act(name, i, g):
            sort_words((name, i, g), t[name, i][:, :, 512 * g : 512 * (g + 1)].bitcast(F32).rearrange("p j (m u) -> p j u m", u=2))

        def sort_err(i, b):
            sort_words(("r", i, b), t["errq", i // 2][:, i % 2, 1024 * b : 1024 * (b + 1)].bitcast(F32).rearrange("p (g m u) -> p g u m", g=2, u=2))

        def turn_act(name, i, g):
            raw = t[name, i]
            if ("sorted", (name, i, g)) in t:
                turn((name, i, g), sorted_words((name, i, g)))
            else:
                turn((name, i, g), second(raw[:, 0, :].bitcast(F32), g) + second(raw[:, 1, :].bitcast(F32), g))

        def evac_act(name, i, g):
            evac((name, i, g))

        def quant_act(name, i, g):
            if name == "aq":
                quant((name, i, g), aq_codes[:, g, 256 * i : 256 * (i + 1)], aq_planes[:, g, 256 * i : 256 * (i + 1)])
            else:
                if g == 0:
                    t["at_codes", i] = work.tile([P, 3, 2 * P], U32, tag="at_codes", name="at_codes", align_bytes=64)
                    t["at_planes", i] = work.tile([P, 3, 2 * P], U8, tag="at_planes", name="at_planes", align_bytes=64)
                quant((name, i, g), t["at_codes", i][:, g, :], t["at_planes", i][:, g, :])

        def mm_act(i):
            acc = psum.tile([P, N], F32, tag="acc", name="acc", bufs=4)
            half = slice(P * (i % 2), P * (i % 2) + P)
            for g in range(3):
                nc.tensor.matmul_mx(
                    out=acc[:], lhsT=t["at_codes", i // 2][:, g, half].bitcast(FP8X4), lhsT_scale=t["at_planes", i // 2][:, g, half],
                    rhs=aq_codes[:, g, :].bitcast(FP8X4), rhs_scale=aq_planes[:, g, :], start=g == 0, stop=g == 2,
                )
            t["gram", i] = acc

        def keep_gram(i):
            nc.scalar.copy(out=gram_act[:, i, :], in_=t["gram", i][:])

        def scale_err(i, h):
            if h == 0:
                t["err", "e", i] = work.tile([P, C], BF16, tag="err", name="err", bufs=3, align_bytes=64)
            k = slice(1024 * h, 1024 * (h + 1))
            nc.vector.tensor_tensor(out=t["err", "e", i][:, k], in0=t["bytes", i // 2][:, i % 2, k].bitcast(FP8), in1=scale[:, k], op=MULT)

        def turn_err(name, i, b):
            words = t["err", "e", i][:].bitcast(F32) if name == "e" else t["errq", i // 2][:, i % 2, :].bitcast(F32)
            if ("sorted", (name, i, b)) in t:
                turn((name, i, b), sorted_words((name, i, b)))
            else:
                turn((name, i, b), second(words, 2 * b) + second(words, 2 * b + 1))

        def evac_err(name, i, b):
            evac((name, i, b))

        def quant_err(name, i, b):
            if b == 0:
                t["codes", name, i] = work.tile([P, 4, P], U32, tag="e_codes", name="e_codes", bufs=3, align_bytes=64)
                t["planes", name, i] = work.tile([P, 4, P], U8, tag="e_planes", name="e_planes", bufs=3, align_bytes=64)
            quant((name, i, b), t["codes", name, i][:, 2 * b : 2 * b + 2, :].rearrange("p g r -> p (g r)"), t["planes", name, i][:, 2 * b : 2 * b + 2, :].rearrange("p g r -> p (g r)"))

        def mm_err(name, i, h):
            acc = psum.tile([P, N], F32, tag="acc", name="acc", bufs=4)
            for g in range(4):
                if name == "e":
                    rhs, rhs_scale = v_codes[:, g, 1024 * h : 1024 * (h + 1)].bitcast(FP4X4), v_planes[:, g, 512 * h : 512 * (h + 1)]
                else:
                    rhs, rhs_scale = w_codes[:, g, 512 * h : 512 * (h + 1)].bitcast(FP8X4), w_planes[:, g, 512 * h : 512 * (h + 1)]
                nc.tensor.matmul_mx(
                    out=acc[:], lhsT=t["codes", name, i][:, g, :].bitcast(FP8X4), lhsT_scale=t["planes", name, i][:, g, :],
                    rhs=rhs, rhs_scale=rhs_scale, start=g == 0, stop=g == 3,
                )
            t["back", name, i, h] = acc

        def slope_mul(name, i, h):
            if h == 0:
                t["d", name, i] = work.tile([P, 2, 2, P, 2], BF16, tag="d", name="d", bufs=3, align_bytes=64)
            nc.vector.tensor_tensor(
                out=t["d", name, i][:, h],
                in0=t["back", name, i, h][:].rearrange("p (m u e) -> p u m e", u=2, e=2),
                in1=t["slope", name, i][:, 512 * h : 512 * (h + 1)].rearrange("p (m u e) -> p u m e", u=2, e=2),
                op=MULT,
            )

        def turn_d(name, i):
            words = t["d", name, i][:].rearrange("p h u m e -> p (h u m e)").bitcast(F32)
            turn(("d", name, i), [words[:, P * j : P * (j + 1)] for j in range(4)])

        def evac_d(name, i):
            evac(("d", name, i))

        def quant_d(name, i):
            if name == "e":
                quant(("d", name, i), dt_codes[:, i].rearrange("p g r -> p (g r)"), dt_planes[:, i].rearrange("p g r -> p (g r)"))
            else:
                x = t["kx", ("d", name, i)]
                for g in range(2):
                    nc.vector.quantize_mx(
                        out=dq_codes[:, g, P * i : P * (i + 1)].bitcast(FP8X4), scales=dq_planes[:, g, P * i : P * (i + 1)],
                        in_=x[:, g].rearrange("p r t -> p (r t)"),
                    )

        def w_lay(c, engine):
            g, n0 = c // 4, 256 * (c % 4)
            x = work.tile([P, 256, 4], BF16, tag="wx", name="wx", bufs=4, align_bytes=64)
            dst = x[:].rearrange("p (c i) t -> p c t i", i=4)
            src = t["w", g][:, :, n0 : n0 + 256].rearrange("p t (c i) -> p c t i", i=4)
            if engine == "act":
                nc.scalar.copy(out=dst, in_=src)
            else:
                nc.vector.tensor_copy(out=dst, in_=src)
            t["wx", c] = x

        def w_quant(c):
            g, n0 = c // 4, 256 * (c % 4)
            nc.vector.quantize_mx(
                out=w_codes[:, g, n0 : n0 + 256].bitcast(FP8X4), scales=w_planes[:, g, n0 : n0 + 256],
                in_=t["wx", c][:].rearrange("p n t -> p (n t)"),
            )

        def mm_gram(i):
            acc = psum.tile([P, N], F32, tag="acc", name="acc", bufs=4)
            for g in range(2):
                nc.tensor.matmul_mx(
                    out=acc[:], lhsT=dt_codes[:, i, g, :].bitcast(FP8X4), lhsT_scale=dt_planes[:, i, g, :],
                    rhs=dq_codes[:, g, :].bitcast(FP8X4), rhs_scale=dq_planes[:, g, :], start=g == 0, stop=g == 1,
                )
            t["ge", i] = acc

        def finish(i):
            res = work.tile([P, N], F32, tag="wx", name="res", bufs=4, align_bytes=64)
            nc.vector.tensor_tensor(out=res[:], in0=t["ge", i][:], in1=gram_act[:, i, :], op=MULT)
            nc.sync.dma_start(out=out[P * i : P * (i + 1), :], in_=res[:])

        for fn, a in [
            (load_act, (act_query, "aq", 0)),
            (load_bytes, (0,)),
            (load_act, (act_query, "aq", 1)),
            (load_act, (act_train, "at", 0)),
            (load_act, (act_train, "at", 1)),
            (load_act, (act_train, "at", 2)),
            (load_w, (0,)),
            (load_bytes, (1,)),
            (load_bytes, (2,)),
            (load_v, ()),
            (load_w, (1,)),
            (load_slope, ("e", 0)),
            (load_err_query, (0,)),
            (load_slope, ("r", 0)),
            (load_act, (act_train, "at", 3)),
            (load_w, (2,)),
            (load_slope, ("e", 1)),
            (load_slope, ("r", 1)),
            (load_err_query, (1,)),
            (load_slope, ("e", 2)),
            (load_bytes, (3,)),
            (load_w, (3,)),
            (load_slope, ("e", 3)),
        ]:
            fn(*a)

        waiting = []
        count = {"lay": 0, "quant": 0}

        def settle(q, n):
            while len(q) > n:
                fn, a = q[0]
                q.remove(q[0])
                fn(*a)

        ORDER = """
            q00 q01 q02 s0a q10 q11 q12 a00 a01 s0b a02 s1a e00 a10 a11 a12 pa s1b s2a a20 e01 wl a21 e10
            s2b A0 A1 a22 wv wq s3a s3b wl e11 e20 A2 wl A3 B00 wq B01 e21 wl s4a e30 e31 wq wq
            s4b wl A4 B10 B11 B20 wq wl pr s5a d0 wq s5b e40 e41 B21 wq wv wl wl pr B30 wq B31
            wq wv wq e50 r00 e51 d1 wq B40 wl wq pr B41 wv r01 wq r10 wl wq wv r11 pr wq d2
            wl wq A5 B50 B51 r20 r21 d3 pa s6a s6b d4 R00 R01 R10 pr pr R11 r30 r31 e60 pa s7a e61
            a30 pa R20 R21 a31 d5 s7b a32 x0 R30 R31 B60 x1 e70 x2 e71 x3 A6 B61 B70 G0 B71 G1 G2
            G3 d6 d7 G4 G5 A7 G6 G7
        """
        using = []
        TURNS = {
            "q": (turn_act, evac_act, quant_act, ("aq",)), "a": (turn_act, evac_act, quant_act, ("at",)),
            "e": (turn_err, evac_err, quant_err, ("e",)), "r": (turn_err, evac_err, quant_err, ("r",)),
            "d": (turn_d, evac_d, quant_d, ("e",)), "x": (turn_d, evac_d, quant_d, ("r",)),
        }
        PRODUCTS = {"A": (mm_act, keep_gram, ()), "B": (mm_err, slope_mul, ("e",)), "R": (mm_err, slope_mul, ("r",)), "G": (mm_gram, finish, ())}
        PREPS = {"q": list(range(6, 6)), "a": list(range(8, 12)), "r": list(range(2, 8))}
        with tc.manual_schedule():
            spread_scale()
            for item in ORDER.split():
                kind = item[0]
                if kind == "p":
                    i = PREPS[item[1]][0]
                    PREPS[item[1]].remove(i)
                    if item[1] == "r":
                        sort_err(i // 2, i % 2)
                    else:
                        sort_act("aq" if item[1] == "q" else "at", i // 3, i % 3)
                elif item in ("wl", "wv"):
                    w_lay(count["lay"], "act" if item == "wl" else "dve")
                    count["lay"] += 1
                elif item == "wq":
                    w_quant(count["quant"])
                    count["quant"] += 1
                elif kind == "s":
                    scale_err(int(item[1]), "ab".index(item[2]))
                elif kind in TURNS:
                    settle(using, 0)
                    turn_fn, evac_fn, quant_fn, first = TURNS[kind]
                    a = first + tuple([int(z) for z in item[1:]])
                    turn_fn(*a)
                    evac_fn(*a)
                    waiting.append((quant_fn, a))
                    settle(waiting, 1)
                else:
                    settle(using, 0)
                    settle(waiting, 0)
                    mm, use, first = PRODUCTS[kind]
                    a = first + tuple([int(z) for z in item[1:]])
                    mm(*a)
                    using.append((use, a))
            settle(using, 0)
